import numpy as np
import ml_dtypes

BF16 = ml_dtypes.bfloat16


def bf(x):
    return np.asarray(x, np.float32).astype(BF16)


def f32(x):
    return np.asarray(x, np.float32)


def f64(x):
    return np.asarray(x).astype(np.float64)


def striped(idx):
    return np.tile(idx.reshape(-1, 16).T, (8, 1))


S, K, M, N, V, D, R = 512, 256, 256, 192, 128, 2, 64


def sigmoid(v):
    return 1.0 / (1.0 + np.exp(-v))


def setup_inputs():
    return {"table": bf(np.random.standard_normal((K, S))), "w": bf(np.random.standard_normal((D, K, M)) / np.sqrt(D * K)), "b": f32(0.5 * np.random.standard_normal((M, 1))), "offs": striped(np.random.permutation(S)[:N])}


def reference(table, w, b, offs):
    idx = offs[:16].T.reshape(-1)
    x = f64(table)[:, idx]
    y = sum(f64(w)[t].T @ x[:, t * R : t * R + V] for t in range(D))
    return (y + f64(b)) * sigmoid(y + f64(b))

@@ -1,0 +1,52 @@
+import concourse.mybir as mybir
+
+P = 128
+K, S = 256, 512
+M, V = 256, 128
+TAPS, REACH = 2, 64
+PER_COLUMN = 16
+
+BF16, F32, U16 = mybir.dt.bfloat16, mybir.dt.float32, mybir.dt.uint16
+SILU = mybir.ActivationFunctionType.Silu
+
+FLOPS = 2 * TAPS * K * M * V
+
+
+def tile_rows_curve_silu_sub_kernel(tc, table, w, b, offs, out):
+    nc = tc.nc
+    k_blocks, m_blocks = K // P, M // P
+    with (
+        tc.tile_pool(name="held", bufs=1) as held,
+        tc.psum_pool(name="psum", bufs=1) as psum,
+    ):
+        offsets = held.tile(list(offs.shape), U16, name="offsets")
+        nc.sync.dma_start(offsets[:], offs)
+
+        points, weights = [], []
+        for kb in range(k_blocks):
+            rows = slice(kb * P, (kb + 1) * P)
+            points.append(held.tile([P, S], BF16, name=f"points{kb}"))
+            nc.sync.dma_start(points[kb][:], table[rows, :])
+            weights.append(held.tile([P, TAPS, M], BF16, name=f"weights{kb}"))
+            nc.scalar.dma_start(weights[kb][:], w[:, rows, :].rearrange("t k m -> k t m"))
+        bias = held.tile([P, m_blocks], F32, name="bias")
+        nc.scalar.dma_start(bias[:], b.rearrange("(mb p) o -> p (mb o)", p=P))
+
+        sums = [psum.tile([P, V], F32, name=f"sums{mb}") for mb in range(m_blocks)]
+        for kb in range(k_blocks):
+            for mb in range(m_blocks):
+                for t in range(TAPS):
+                    first_column = t * REACH // PER_COLUMN
+                    picked = points[kb][:].indirect(offsets[:, first_column : first_column + V // PER_COLUMN])
+                    nc.tensor.matmul(
+                        sums[mb][:],
+                        weights[kb][:, t, mb * P : (mb + 1) * P],
+                        picked,
+                        start=(kb == 0 and t == 0),
+                        stop=(kb == k_blocks - 1 and t == TAPS - 1),
+                    )
+
+        for mb in range(m_blocks):
+            result = held.tile([P, V], F32, name=f"result{mb}")
+            nc.scalar.activation(result[:], sums[mb][:], SILU, bias=bias[:, mb : mb + 1])
+            nc.sync.dma_start(out[mb * P : (mb + 1) * P, :], result[:])

@@ -32,6 +32,11 @@ def tile_rows_curve_silu_sub_kernel(tc, table, w, b, offs, out):
         bias = held.tile([P, m_blocks], F32, name="bias")
         nc.scalar.dma_start(bias[:], b.rearrange("(mb p) o -> p (mb o)", p=P))
 
+        idle_in = held.tile([P, 1], F32, name="idle_in")
+        idle_out = held.tile([P, 1], F32, name="idle_out")
+        nc.vector.memset(idle_in[:], 0.0)
+        nc.scalar.activation(idle_out[:], idle_in[:], SILU)
+
         sums = [psum.tile([P, V], F32, name=f"sums{mb}") for mb in range(m_blocks)]
         for kb in range(k_blocks):
             for mb in range(m_blocks):

import concourse.mybir as mybir

P = 128
K, S = 256, 512
M, V = 256, 128
TAPS, REACH = 2, 64
PER_COLUMN = 16

BF16, F32, U16 = mybir.dt.bfloat16, mybir.dt.float32, mybir.dt.uint16
SILU = mybir.ActivationFunctionType.Silu

FLOPS = 2 * TAPS * K * M * V


def tile_rows_curve_silu_sub_kernel(tc, table, w, b, offs, out):
    nc = tc.nc
    k_blocks, m_blocks = K // P, M // P
    with (
        tc.tile_pool(name="held", bufs=1) as held,
        tc.psum_pool(name="psum", bufs=1) as psum,
    ):
        offsets = held.tile(list(offs.shape), U16, name="offsets")
        nc.sync.dma_start(offsets[:], offs)

        points, weights = [], []
        for kb in range(k_blocks):
            rows = slice(kb * P, (kb + 1) * P)
            points.append(held.tile([P, S], BF16, name=f"points{kb}"))
            nc.sync.dma_start(points[kb][:], table[rows, :])
            weights.append(held.tile([P, TAPS, M], BF16, name=f"weights{kb}"))
            nc.scalar.dma_start(weights[kb][:], w[:, rows, :].rearrange("t k m -> k t m"))
        bias = held.tile([P, m_blocks], F32, name="bias")
        nc.scalar.dma_start(bias[:], b.rearrange("(mb p) o -> p (mb o)", p=P))

        idle_in = held.tile([P, 1], F32, name="idle_in")
        idle_out = held.tile([P, 1], F32, name="idle_out")
        nc.vector.memset(idle_in[:], 0.0)
        nc.scalar.activation(idle_out[:], idle_in[:], SILU)

        sums = [psum.tile([P, V], F32, name=f"sums{mb}") for mb in range(m_blocks)]
        for kb in range(k_blocks):
            for mb in range(m_blocks):
                for t in range(TAPS):
                    first_column = t * REACH // PER_COLUMN
                    picked = points[kb][:].indirect(offsets[:, first_column : first_column + V // PER_COLUMN])
                    nc.tensor.matmul(
                        sums[mb][:],
                        weights[kb][:, t, mb * P : (mb + 1) * P],
                        picked,
                        start=(kb == 0 and t == 0),
                        stop=(kb == k_blocks - 1 and t == TAPS - 1),
                    )

        for mb in range(m_blocks):
            result = held.tile([P, V], F32, name=f"result{mb}")
            nc.scalar.activation(result[:], sums[mb][:], SILU, bias=bias[:, mb : mb + 1])
            nc.sync.dma_start(out[mb * P : (mb + 1) * P, :], result[:])
